import numpy as np
import ml_dtypes


def mxq(x, axis, fmt="e4m3"):
    dtype, down = {"e4m3": (ml_dtypes.float8_e4m3fn, 7), "e5m2": (ml_dtypes.float8_e5m2, 14)}[fmt]
    v = np.moveaxis(np.asarray(x, np.float32).astype(ml_dtypes.bfloat16).astype(np.float64), axis, -1)
    blocks = v.reshape(v.shape[:-1] + (-1, 32))
    amax = np.abs(blocks).max(-1, keepdims=True)
    byte = np.maximum(np.where(amax > 0, np.frexp(amax)[1] - 1 + 127, 0) - down, 1)
    scale = np.exp2(byte - 127.0)
    codes = (blocks / scale).astype(np.float32).astype(dtype).astype(np.float64)
    return np.moveaxis((codes * scale).reshape(v.shape), -1, axis)


WIDE = False


def mx_kscale(k):
    if not WIDE:
        return np.ones(k)
    levels = np.array([10, -10, 5, -5, 0])
    if k % 512:
        return np.exp2(np.random.permutation(np.resize(levels, k // 32))).repeat(32)
    a = np.empty((k // 512, 16))
    for p in range(k // 512):
        a[p, :8] = np.random.permutation(np.resize(levels, 8))
        for g in range(8):
            far = levels[np.abs(levels - a[p, g]) >= 10]
            a[p, g + 8] = far[np.random.randint(len(far))]
    return np.exp2(a.ravel()).repeat(32)


def f64(x):
    return np.asarray(x).astype(np.float64)


def striped(idx):
    return np.tile(idx.reshape(-1, 16).T, (8, 1)).astype(np.uint16)


def unstriped(offs):
    return offs[:16].T.reshape(-1).astype(np.int64)


def striped8(idx):
    return np.concatenate([x.reshape(-1, 16).T for x in idx]).astype(np.uint16)


def runs(offs, k):
    lists = np.stack([offs[16 * r : 16 * r + 16].T.reshape(-1) for r in range(8)]).astype(np.int64)
    return lists[np.arange(k) % 512 // 64]


def pack_weight(w):
    k, n = w.shape
    w = f64(np.asarray(w, np.float32).astype(ml_dtypes.bfloat16)).reshape(k // 32, 32, n)
    amax = np.abs(w).max(1)
    byte = np.clip(np.where(amax > 0, np.frexp(amax)[1] - 1 + 127 - 7, 1), 1, 254)
    scaled = (w * np.exp2(127.0 - byte)[:, None, :]).reshape(k, n).astype(np.float32)
    words = np.ascontiguousarray(scaled.reshape(k // 512, 128, 4, n).transpose(0, 1, 3, 2)).astype(ml_dtypes.float8_e4m3fn).view(np.uint8)
    return words, np.ascontiguousarray(byte.astype(np.uint8).reshape(k // 512, 16, n))


def unpack_weight(words, scales):
    g, p, n, _ = words.shape
    vals = np.ascontiguousarray(words).view(ml_dtypes.float8_e4m3fn).astype(np.float64) * np.repeat(np.exp2(scales.astype(np.float64) - 127.0), 8, axis=1)[..., None]
    return vals.transpose(0, 1, 3, 2).reshape(g * 512, n)

def planes(y):
    n, m = y.shape
    v = y.astype(np.float32).astype(ml_dtypes.bfloat16).astype(np.float64).reshape(n // 32, 32, m)
    top = np.abs(v).max(1)
    byte = np.clip(np.where(top > 0, np.frexp(top)[1] - 1 + 127 - 7, 1), 1, 254)
    codes = (v * np.exp2(127.0 - byte)[:, None, :]).reshape(n, m).astype(np.float32).astype(ml_dtypes.float8_e4m3fn).view(np.uint8)
    words = codes.reshape(n // 512, 128, 4, m).transpose(0, 1, 3, 2)
    return np.ascontiguousarray(words), np.ascontiguousarray(byte.astype(np.uint8).reshape(n // 512, 16, m))


K, T, S, H, C = 512, 2048, 512, 512, 512
P = 2 ** 7


def setup_inputs():
    n = np.random.standard_normal
    s = mx_kscale(K)[:, None]
    packed_xT = pack_weight(n((K, T)) * s)
    packed_w1 = pack_weight(n((K, H)) / np.sqrt(K) / s)
    packed_w2 = pack_weight(n((K, H)) / np.sqrt(K) / s)
    return {
        "x_words": packed_xT[0],
        "x_scales": packed_xT[1],
        "w1_words": packed_w1[0],
        "w1_scales": packed_w1[1],
        "w2_words": packed_w2[0],
        "w2_scales": packed_w2[1],
        "tr1": np.tile(np.random.uniform(-1, 1, S), (P, 1)).astype(np.float32),
        "tr2": np.tile(np.random.uniform(-1, 1, S), (P, 1)).astype(np.float32),
        "tr3": np.tile(np.random.uniform(-1, 1, S), (P, 1)).astype(np.float32),
        "gs": (np.random.uniform(0.5, 1.5, (K, 1)) / s).astype(np.float32),
        "offs": striped(np.random.permutation(T)[:S]),
        "two": striped(np.random.permutation(T)[:S]),
        "s1": striped8(np.stack([np.random.permutation(S) for _ in range(8)])),
        "s2": striped8(np.stack([np.random.permutation(S) for _ in range(8)])),
        "s3": striped8(np.stack([np.random.permutation(S) for _ in range(8)])),
        "cand": striped(np.random.permutation(T)[:C]),
    }


def reference(x_words, x_scales, w1_words, w1_scales, w2_words, w2_scales, tr1, tr2, tr3, gs, offs, two, s1, s2, s3, cand):
    x_cand = unpack_weight(x_words, x_scales)[:, unstriped(cand)]
    x_two = unpack_weight(x_words, x_scales)[:, unstriped(two)]
    c = unpack_weight(w2_words, w2_scales).T @ x_two
    xq = unpack_weight(x_words, x_scales)[:, unstriped(offs)]
    y = unpack_weight(w1_words, w1_scales).T @ xq
    z = f64(gs) * (c + np.maximum(np.maximum(y[np.arange(H)[:, None], runs(s1, H)] + f64(tr1)[:1], y[np.arange(H)[:, None], runs(s2, H)] + f64(tr2)[:1]), y[np.arange(H)[:, None], runs(s3, H)] + f64(tr3)[:1]))
    out_0 = 0.0625 * ((x_cand.T @ mxq(z, 0, "e4m3")))
    return (out_0,) + planes(out_0)

@@ -1,0 +1,171 @@
+from contextlib import ExitStack
+
+import concourse.mybir as mybir
+
+F32 = mybir.dt.float32
+BF16 = mybir.dt.bfloat16
+I32 = mybir.dt.int32
+U32 = mybir.dt.uint32
+U16 = mybir.dt.uint16
+U8 = mybir.dt.uint8
+FP8X4 = mybir.dt.float8_e4m3fn_x4
+ALU = mybir.AluOpType
+COPY = mybir.ActivationFunctionType.Copy
+
+P = 128
+PACK = 4
+T = 2048
+S = 512
+UNIT = 128
+CHUNKS = ((0, 256), (256, 128), (384, 128))
+FLOPS = 3 * 2 * 512 * 512 * 512
+
+
+def tile_picked_viterb3_none_po_kernel(tc, x_words, x_scales, w1_words, w1_scales, w2_words, w2_scales, tr1, tr2, tr3, gs, offs, two, s1, s2, s3, cand, out_0, out_1, out_2):
+    nc = tc.nc
+
+    def words_of(ap):
+        return ap[0].rearrange("p n t -> p (n t)").bitcast(I32)
+
+    def dealt(ap):
+        return ap.rearrange("p (t m) -> p m t", t=PACK)
+
+    def plain(ap):
+        return ap.rearrange("p (m t) -> p m t", t=PACK)
+
+    with ExitStack() as ctx:
+        lists = ctx.enter_context(tc.tile_pool(name="lists", bufs=1))
+        keep = ctx.enter_context(tc.tile_pool(name="keep", bufs=1))
+        work = ctx.enter_context(tc.tile_pool(name="work", bufs=3))
+        psum = ctx.enter_context(tc.psum_pool(name="psum", bufs=8))
+
+        def new_list(name):
+            return lists.tile([P, S // 16], U16, name=name)
+
+        def held(shape, dtype, name):
+            return keep.tile(shape, dtype, name=name, align_bytes=64)
+
+        offs_l, two_l, cand_l = new_list("offs_l"), new_list("two_l"), new_list("cand_l")
+        s_l = [new_list("s1_l"), new_list("s2_l"), new_list("s3_l")]
+        xw = held([P, T], U32, "xw")
+        xs = held([P, T], U8, "xs")
+        w_raw = [held([P, S], U32, "w1_raw"), held([P, S], U32, "w2_raw")]
+        ws_raw = held([P, S], U8, "ws_raw")
+        tr = [held([P, S], F32, "tr1_t"), held([P, S], F32, "tr2_t"), held([P, S], F32, "tr3_t")]
+        gain = held([P, PACK], F32, "gain")
+
+        nc.vector.memset(xs[:].bitcast(I32), 0)
+        nc.gpsimd.memset(ws_raw[:].bitcast(I32), 0)
+        for q in range(4):
+            nc.sync.dma_start(xs[32 * q : 32 * q + 4, :].bitcast(I32), x_scales[0, 4 * q : 4 * q + 4, :].bitcast(I32))
+        nc.sync.dma_start(offs_l[:], offs)
+        nc.sync.dma_start(two_l[:], two)
+        nc.sync.dma_start(cand_l[:], cand)
+        nc.sync.dma_start(xw[:].bitcast(I32), words_of(x_words))
+        nc.sync.dma_start(w_raw[0][:].bitcast(I32), words_of(w1_words))
+        for i, scales in enumerate((w1_scales, w2_scales)):
+            for q in range(4):
+                nc.sync.dma_start(ws_raw[32 * q + 4 * i : 32 * q + 4 * i + 4, :].bitcast(I32), scales[0, 4 * q : 4 * q + 4, :].bitcast(I32))
+        nc.sync.dma_start(w_raw[1][:].bitcast(I32), words_of(w2_words))
+        for tile, src in zip(s_l, (s1, s2, s3)):
+            nc.sync.dma_start(tile[:], src)
+        for tile, src in zip(tr, (tr1, tr2, tr3)):
+            nc.sync.dma_start(tile[:], src)
+        nc.sync.dma_start(gain[:], gs.rearrange("(p t) o -> p (t o)", t=PACK))
+
+        picked_w = [held([P, S], U32, "offs_w"), held([P, S], U32, "two_w"), held([P, S], U32, "cand_w")]
+        picked_s = [held([P, S], U8, "offs_s"), held([P, S], U8, "two_s"), held([P, S], U8, "cand_s")]
+        order = (offs_l, two_l, cand_l)
+        w_dealt = [held([P, S], U32, "w1_dealt"), held([P, S], U32, "w2_dealt")]
+        ws_dealt = held([P, S], U8, "ws_dealt")
+        cand_wd = held([P, S], U32, "cand_wd")
+        cand_sd = held([P, S], U8, "cand_sd")
+
+        for i in range(3):
+            nc.vector.tensor_copy(picked_s[i][:], xs[:].indirect(order[i][:]))
+        nc.vector.tensor_copy(picked_w[0][:], xw[:].indirect(offs_l[:]))
+        nc.vector.tensor_copy(dealt(w_dealt[0][:]), plain(w_raw[0][:]))
+        nc.vector.tensor_copy(dealt(ws_dealt[:]), plain(ws_raw[:]))
+
+        y = [held([P, S], F32, "y%d" % t) for t in range(PACK)]
+        cg = [held([P, S], F32, "cg%d" % t) for t in range(PACK)]
+        for t in range(PACK):
+            cols = slice(t * P, (t + 1) * P)
+            bank = psum.tile([P, S], F32, name="bank")
+            nc.tensor.matmul_mx(out=bank[:], lhsT=w_dealt[0][:, cols].bitcast(FP8X4), lhsT_scale=ws_dealt[:, cols],
+                                rhs=picked_w[0][:].bitcast(FP8X4), rhs_scale=picked_s[0][:], start=True, stop=True)
+            nc.scalar.activation(y[t][:], bank[:], COPY)
+
+        nc.vector.tensor_copy(picked_w[1][:], xw[:].indirect(two_l[:]))
+        nc.vector.tensor_copy(dealt(w_dealt[1][:]), plain(w_raw[1][:]))
+        for t in range(PACK):
+            cols = slice(t * P, (t + 1) * P)
+            bank = psum.tile([P, S], F32, name="bank")
+            nc.tensor.matmul_mx(out=bank[:], lhsT=w_dealt[1][:, cols].bitcast(FP8X4), lhsT_scale=ws_dealt[4:P, cols],
+                                rhs=picked_w[1][:].bitcast(FP8X4), rhs_scale=picked_s[1][:], start=True, stop=True)
+            nc.scalar.activation(cg[t][:], bank[:], COPY, scale=gain[:, t : t + 1])
+        nc.vector.tensor_copy(picked_w[2][:], xw[:].indirect(cand_l[:]))
+        nc.vector.tensor_copy(dealt(cand_sd[:]), plain(picked_s[2][:]))
+        nc.vector.tensor_copy(dealt(cand_wd[:]), plain(picked_w[2][:]))
+
+        z_words = held([P, S], U32, "z_words")
+        z_scales = held([P, S], U8, "z_scales")
+        o_words = held([P, S], U32, "o_words")
+        o_scales = held([P, S], U8, "o_scales")
+        out_rows = out_0.rearrange("(p t) j -> p t j", t=PACK)
+        out_words = words_of(out_1)
+
+        def trellis(j0, n):
+            cols = slice(j0, j0 + n)
+            z = work.tile([P, PACK, n], F32, name="z")
+            reach = [work.tile([P, PACK, n], F32, name="reach%d" % k) for k in range(3)]
+            steps = []
+            for t in range(PACK):
+                def fetch(k, t=t):
+                    nc.vector.tensor_tensor(reach[k][:, t, :], y[t][:].indirect(s_l[k][:, j0 // 16 : (j0 + n) // 16]), tr[k][:, cols], ALU.add)
+
+                def best(k, t=t):
+                    nc.vector.tensor_tensor(reach[0][:, t, :], reach[0][:, t, :], reach[k][:, t, :], ALU.max)
+
+                def weigh(t=t):
+                    nc.vector.scalar_tensor_tensor(z[:, t, :], reach[0][:, t, :], gain[:, t : t + 1], cg[t][:, cols], ALU.mult, ALU.add)
+
+                steps.append((fetch, best, weigh))
+            for t in range(PACK + 1):
+                if t < PACK:
+                    steps[t][0](0)
+                if t > 0:
+                    steps[t - 1][1](2)
+                if t < PACK:
+                    steps[t][0](1)
+                if t > 0:
+                    steps[t - 1][2]()
+                if t < PACK:
+                    steps[t][0](2)
+                    steps[t][1](1)
+            return z
+
+        def score(z, j0, u0):
+            cols = slice(j0 + u0, j0 + u0 + UNIT)
+            zb = work.tile([P, UNIT, PACK], BF16, name="zb", align_bytes=64)
+            nc.scalar.copy(zb[:].rearrange("p (c i) t -> p c t i", i=4), z[:, :, u0 : u0 + UNIT].rearrange("p t (c i) -> p c t i", i=4))
+            nc.vector.quantize_mx(out=z_words[:, cols].bitcast(FP8X4), scales=z_scales[:, cols], in_=zb[:].rearrange("p j t -> p (j t)"))
+            bank = psum.tile([P, PACK, UNIT], F32, name="bank")
+            for t in range(PACK):
+                rows = slice(t * P, (t + 1) * P)
+                nc.tensor.matmul_mx(out=bank[:, t, :], lhsT=cand_wd[:, rows].bitcast(FP8X4), lhsT_scale=cand_sd[:, rows],
+                                    rhs=z_words[:, cols].bitcast(FP8X4), rhs_scale=z_scales[:, cols], start=True, stop=True)
+            ob = work.tile([P, UNIT, PACK], BF16, name="ob", align_bytes=64)
+            nc.scalar.activation(ob[:], bank[:].rearrange("p t j -> p j t"), COPY, scale=0.0625)
+            of = work.tile([P, PACK, UNIT], F32, name="of")
+            nc.scalar.activation(of[:], bank[:], COPY, scale=0.0625)
+            nc.sync.dma_start(out_rows[:, :, cols], of[:])
+            nc.vector.quantize_mx(out=o_words[:, cols].bitcast(FP8X4), scales=o_scales[:, cols], in_=ob[:].rearrange("p j t -> p (j t)"))
+            nc.sync.dma_start(out_words[:, cols], o_words[:, cols].bitcast(I32))
+
+        for j0, n in CHUNKS:
+            z = trellis(j0, n)
+            for u0 in range(0, n, UNIT):
+                score(z, j0, u0)
+        for q in range(4):
+            nc.sync.dma_start(out_2[0, 4 * q : 4 * q + 4, :].bitcast(I32), o_scales[32 * q : 32 * q + 4, :].bitcast(I32))

@@ -1,6 +1,7 @@
 from contextlib import ExitStack
 
 import concourse.mybir as mybir
+from concourse.masks import make_identity
 
 F32 = mybir.dt.float32
 BF16 = mybir.dt.bfloat16
@@ -11,13 +12,15 @@ U8 = mybir.dt.uint8
 FP8X4 = mybir.dt.float8_e4m3fn_x4
 ALU = mybir.AluOpType
 COPY = mybir.ActivationFunctionType.Copy
+IDENTITY = mybir.ActivationFunctionType.Identity
+RELU = mybir.ActivationFunctionType.Relu
 
 P = 128
 PACK = 4
 T = 2048
 S = 512
 UNIT = 128
-CHUNKS = ((0, 256), (256, 128), (384, 128))
+UNITS = S // UNIT
 FLOPS = 3 * 2 * 512 * 512 * 512
 
 
@@ -36,8 +39,9 @@ def tile_picked_viterb3_none_po_kernel(tc, x_words, x_scales, w1_words, w1_scale
     with ExitStack() as ctx:
         lists = ctx.enter_context(tc.tile_pool(name="lists", bufs=1))
         keep = ctx.enter_context(tc.tile_pool(name="keep", bufs=1))
-        work = ctx.enter_context(tc.tile_pool(name="work", bufs=3))
-        psum = ctx.enter_context(tc.psum_pool(name="psum", bufs=8))
+        work = ctx.enter_context(tc.tile_pool(name="work", bufs=2))
+        psum = ctx.enter_context(tc.psum_pool(name="psum", bufs=5))
+        turns = ctx.enter_context(tc.psum_pool(name="turns", bufs=1))
 
         def new_list(name):
             return lists.tile([P, S // 16], U16, name=name)
@@ -45,68 +49,97 @@ def tile_picked_viterb3_none_po_kernel(tc, x_words, x_scales, w1_words, w1_scale
         def held(shape, dtype, name):
             return keep.tile(shape, dtype, name=name, align_bytes=64)
 
+        def tagged(shape, dtype, name, tag):
+            return keep.tile(shape, dtype, name=name, tag=tag, align_bytes=64)
+
         offs_l, two_l, cand_l = new_list("offs_l"), new_list("two_l"), new_list("cand_l")
         s_l = [new_list("s1_l"), new_list("s2_l"), new_list("s3_l")]
         xw = held([P, T], U32, "xw")
         xs = held([P, T], U8, "xs")
-        w_raw = [held([P, S], U32, "w1_raw"), held([P, S], U32, "w2_raw")]
-        ws_raw = held([P, S], U8, "ws_raw")
-        tr = [held([P, S], F32, "tr1_t"), held([P, S], F32, "tr2_t"), held([P, S], F32, "tr3_t")]
+        w1_raw, w2_raw = held([P, S], U32, "w1_raw"), held([P, S], U32, "w2_raw")
+        w1s_raw, w2s_raw = held([P, S], U8, "w1s_raw"), held([P, S], U8, "w2s_raw")
+        tr_rows = held([P, P], F32, "tr_rows")
         gain = held([P, PACK], F32, "gain")
 
-        nc.vector.memset(xs[:].bitcast(I32), 0)
-        nc.gpsimd.memset(ws_raw[:].bitcast(I32), 0)
-        for q in range(4):
-            nc.sync.dma_start(xs[32 * q : 32 * q + 4, :].bitcast(I32), x_scales[0, 4 * q : 4 * q + 4, :].bitcast(I32))
+        def load_scales(tile, scales):
+            for q in range(4):
+                nc.sync.dma_start(tile[32 * q : 32 * q + 4, :].bitcast(I32), scales[0, 4 * q : 4 * q + 4, :].bitcast(I32))
+
+        nc.gpsimd.memset(xs[:].bitcast(I32), 0)
+        nc.vector.memset(w1s_raw[:].bitcast(I32), 0)
+        nc.vector.memset(tr_rows[:], 0.0)
+        nc.vector.memset(w2s_raw[:].bitcast(I32), 0)
+        ident = held([P, P], F32, "ident")
+        make_identity(nc, ident[:])
+        nc.sync.dma_start(w1_raw[:].bitcast(I32), words_of(w1_words))
+        load_scales(xs, x_scales)
         nc.sync.dma_start(offs_l[:], offs)
         nc.sync.dma_start(two_l[:], two)
-        nc.sync.dma_start(cand_l[:], cand)
         nc.sync.dma_start(xw[:].bitcast(I32), words_of(x_words))
-        nc.sync.dma_start(w_raw[0][:].bitcast(I32), words_of(w1_words))
-        for i, scales in enumerate((w1_scales, w2_scales)):
-            for q in range(4):
-                nc.sync.dma_start(ws_raw[32 * q + 4 * i : 32 * q + 4 * i + 4, :].bitcast(I32), scales[0, 4 * q : 4 * q + 4, :].bitcast(I32))
-        nc.sync.dma_start(w_raw[1][:].bitcast(I32), words_of(w2_words))
-        for tile, src in zip(s_l, (s1, s2, s3)):
-            nc.sync.dma_start(tile[:], src)
-        for tile, src in zip(tr, (tr1, tr2, tr3)):
-            nc.sync.dma_start(tile[:], src)
+        for k, scores in enumerate((tr1, tr2, tr3)):
+            nc.sync.dma_start(tr_rows[UNITS * k : UNITS * (k + 1), :], scores[0:1, :].rearrange("o (u j) -> (o u) j", j=UNIT))
+        load_scales(w1s_raw, w1_scales)
+        nc.sync.dma_start(cand_l[:], cand)
+        nc.sync.dma_start(s_l[0][:], s1)
+        nc.sync.dma_start(w2_raw[:].bitcast(I32), words_of(w2_words))
+        load_scales(w2s_raw, w2_scales)
+        nc.sync.dma_start(s_l[1][:], s2)
+        nc.sync.dma_start(s_l[2][:], s3)
         nc.sync.dma_start(gain[:], gs.rearrange("(p t) o -> p (t o)", t=PACK))
 
-        picked_w = [held([P, S], U32, "offs_w"), held([P, S], U32, "two_w"), held([P, S], U32, "cand_w")]
-        picked_s = [held([P, S], U8, "offs_s"), held([P, S], U8, "two_s"), held([P, S], U8, "cand_s")]
-        order = (offs_l, two_l, cand_l)
-        w_dealt = [held([P, S], U32, "w1_dealt"), held([P, S], U32, "w2_dealt")]
-        ws_dealt = held([P, S], U8, "ws_dealt")
+        offs_w, two_w, cand_w = held([P, S], U32, "offs_w"), held([P, S], U32, "two_w"), held([P, S], U32, "cand_w")
+        offs_s, two_s, cand_s = held([P, S], U8, "offs_s"), held([P, S], U8, "two_s"), held([P, S], U8, "cand_s")
+        w1_dealt = held([P, S], U32, "w1_dealt")
+        w1s_dealt = held([P, S], U8, "w1s_dealt")
         cand_wd = held([P, S], U32, "cand_wd")
         cand_sd = held([P, S], U8, "cand_sd")
 
-        for i in range(3):
-            nc.vector.tensor_copy(picked_s[i][:], xs[:].indirect(order[i][:]))
-        nc.vector.tensor_copy(picked_w[0][:], xw[:].indirect(offs_l[:]))
-        nc.vector.tensor_copy(dealt(w_dealt[0][:]), plain(w_raw[0][:]))
-        nc.vector.tensor_copy(dealt(ws_dealt[:]), plain(ws_raw[:]))
+        nc.vector.tensor_copy(dealt(w1_dealt[:]), plain(w1_raw[:]))
+        nc.vector.tensor_copy(offs_s[:], xs[:].indirect(offs_l[:]))
+        nc.vector.tensor_copy(two_s[:], xs[:].indirect(two_l[:]))
+        nc.vector.tensor_copy(offs_w[:], xw[:].indirect(offs_l[:]))
+        nc.vector.tensor_copy(dealt(w1s_dealt[:]), plain(w1s_raw[:]))
+        nc.vector.tensor_copy(two_w[:], xw[:].indirect(two_l[:]))
+
+        bank = turns.tile([P, P], F32, name="turn", tag="turn0")
+        nc.tensor.transpose(bank[:], tr_rows[:], ident[:])
+        last_cols = held([P, UNITS], F32, "last_cols")
+        minus_last = held([P, UNITS], F32, "minus_last")
+        lead_cols = held([P, 2 * UNITS], F32, "lead_cols")
+        nc.scalar.activation(minus_last[:], bank[:, 2 * UNITS : 3 * UNITS], COPY, scale=-1.0)
+        nc.scalar.copy(last_cols[:], bank[:, 2 * UNITS : 3 * UNITS])
+        for u in range(UNITS):
+            nc.scalar.activation(lead_cols[:, u : 2 * UNITS : UNITS], bank[:, u : 2 * UNITS : UNITS], IDENTITY, bias=minus_last[:, u : u + 1])
+        lead = []
+        for k in range(2):
+            bank = turns.tile([P, S], F32, name="turn", tag="turn%d" % (k + 1))
+            for u in range(UNITS):
+                column = lead_cols[:, UNITS * k + u : UNITS * k + u + 1]
+                nc.tensor.transpose(bank[:, u * UNIT : (u + 1) * UNIT], column.to_broadcast([P, P]), ident[:])
+            lead.append(held([P, S], F32, "lead%d" % k))
+            nc.scalar.copy(lead[k][:], bank[:])
 
         y = [held([P, S], F32, "y%d" % t) for t in range(PACK)]
-        cg = [held([P, S], F32, "cg%d" % t) for t in range(PACK)]
         for t in range(PACK):
             cols = slice(t * P, (t + 1) * P)
             bank = psum.tile([P, S], F32, name="bank")
-            nc.tensor.matmul_mx(out=bank[:], lhsT=w_dealt[0][:, cols].bitcast(FP8X4), lhsT_scale=ws_dealt[:, cols],
-                                rhs=picked_w[0][:].bitcast(FP8X4), rhs_scale=picked_s[0][:], start=True, stop=True)
-            nc.scalar.activation(y[t][:], bank[:], COPY)
+            nc.tensor.matmul_mx(out=bank[:], lhsT=w1_dealt[:, cols].bitcast(FP8X4), lhsT_scale=w1s_dealt[:, cols],
+                                rhs=offs_w[:].bitcast(FP8X4), rhs_scale=offs_s[:], start=True, stop=True)
+            nc.scalar.copy(y[t][:], bank[:])
 
-        nc.vector.tensor_copy(picked_w[1][:], xw[:].indirect(two_l[:]))
-        nc.vector.tensor_copy(dealt(w_dealt[1][:]), plain(w_raw[1][:]))
-        for t in range(PACK):
-            cols = slice(t * P, (t + 1) * P)
+        emit = []
+        for u in range(UNITS):
+            cols = slice(u * UNIT, (u + 1) * UNIT)
             bank = psum.tile([P, S], F32, name="bank")
-            nc.tensor.matmul_mx(out=bank[:], lhsT=w_dealt[1][:, cols].bitcast(FP8X4), lhsT_scale=ws_dealt[4:P, cols],
-                                rhs=picked_w[1][:].bitcast(FP8X4), rhs_scale=picked_s[1][:], start=True, stop=True)
-            nc.scalar.activation(cg[t][:], bank[:], COPY, scale=gain[:, t : t + 1])
-        nc.vector.tensor_copy(picked_w[2][:], xw[:].indirect(cand_l[:]))
-        nc.vector.tensor_copy(dealt(cand_sd[:]), plain(picked_s[2][:]))
-        nc.vector.tensor_copy(dealt(cand_wd[:]), plain(picked_w[2][:]))
+            nc.tensor.matmul_mx(out=bank[:], lhsT=two_w[:, cols].bitcast(FP8X4), lhsT_scale=two_s[:, cols],
+                                rhs=w2_raw[:].bitcast(FP8X4), rhs_scale=w2s_raw[:], start=True, stop=True)
+            emit.append(held([P, PACK, P], F32, "emit%d" % u))
+            nc.scalar.activation(emit[u][:], bank[:].rearrange("j (p t) -> j t p", t=PACK), IDENTITY, bias=last_cols[:, u : u + 1])
+
+        nc.vector.tensor_copy(cand_s[:], xs[:].indirect(cand_l[:]))
+        nc.vector.tensor_copy(cand_w[:], xw[:].indirect(cand_l[:]))
+        nc.vector.tensor_copy(dealt(cand_sd[:]), plain(cand_s[:]))
+        nc.vector.tensor_copy(dealt(cand_wd[:]), plain(cand_w[:]))
 
         z_words = held([P, S], U32, "z_words")
         z_scales = held([P, S], U8, "z_scales")
@@ -115,57 +148,111 @@ def tile_picked_viterb3_none_po_kernel(tc, x_words, x_scales, w1_words, w1_scale
         out_rows = out_0.rearrange("(p t) j -> p t j", t=PACK)
         out_words = words_of(out_1)
 
-        def trellis(j0, n):
-            cols = slice(j0, j0 + n)
-            z = work.tile([P, PACK, n], F32, name="z")
-            reach = [work.tile([P, PACK, n], F32, name="reach%d" % k) for k in range(3)]
-            steps = []
+        def window(k, t, u):
+            return y[t][:].indirect(s_l[k][:, u * UNIT // 16 : (u + 1) * UNIT // 16])
+
+        def new_room(u):
+            return tagged([P, 3, PACK, UNIT], F32, "room", "pairs%d" % max(u - 2, -1))
+
+        room = {0: new_room(0)}
+
+        def best_of_two(u, then):
+            cols = slice(u * UNIT, (u + 1) * UNIT)
+            a, b = room[u][:, 0], room[u][:, 1]
             for t in range(PACK):
-                def fetch(k, t=t):
-                    nc.vector.tensor_tensor(reach[k][:, t, :], y[t][:].indirect(s_l[k][:, j0 // 16 : (j0 + n) // 16]), tr[k][:, cols], ALU.add)
+                nc.vector.tensor_tensor(a[:, t, :], window(0, t, u), lead[0][:, cols], ALU.add)
+            for t in range(PACK):
+                if t == PACK - 1:
+                    nc.vector.tensor_tensor(a[:, 0:2, :], a[:, 0:2, :], b[:, 0:2, :], ALU.max)
+                nc.vector.tensor_tensor(b[:, t, :], window(1, t, u), lead[1][:, cols], ALU.add)
+            then(b, 0)
+            nc.vector.tensor_tensor(a[:, 2:4, :], a[:, 2:4, :], b[:, 2:4, :], ALU.max)
+            for t in range(1, PACK):
+                then(b, t)
 
-                def best(k, t=t):
-                    nc.vector.tensor_tensor(reach[0][:, t, :], reach[0][:, t, :], reach[k][:, t, :], ALU.max)
+        def turn(src, side):
+            bank = turns.tile([P, PACK, P], F32, name="turn", tag="turn%d" % side)
+            for t in range(PACK):
+                nc.tensor.transpose(bank[:, t, :], src[:, t, :], ident[:])
+            return bank
 
-                def weigh(t=t):
-                    nc.vector.scalar_tensor_tensor(z[:, t, :], reach[0][:, t, :], gain[:, t : t + 1], cg[t][:, cols], ALU.mult, ALU.add)
+        def add_turned(total, term, opens, closes):
+            for t in range(PACK):
+                nc.tensor.matmul(total[:, t, :], term[:, t, :], ident[:], start=(opens and t == 0), stop=(closes and t == PACK - 1), is_transpose=True)
 
-                steps.append((fetch, best, weigh))
-            for t in range(PACK + 1):
-                if t < PACK:
-                    steps[t][0](0)
-                if t > 0:
-                    steps[t - 1][1](2)
-                if t < PACK:
-                    steps[t][0](1)
-                if t > 0:
-                    steps[t - 1][2]()
-                if t < PACK:
-                    steps[t][0](2)
-                    steps[t][1](1)
-            return z
+        def trellis(u):
+            total = turns.tile([P, PACK, UNIT], F32, name="total", tag="turn%d" % (u % 3))
+            add_turned(total, emit[u], True, False)
+            excess = tagged([P, PACK, UNIT], F32, "excess", "excess%d" % u)
+            a = room[u][:, 0]
 
-        def score(z, j0, u0):
-            cols = slice(j0 + u0, j0 + u0 + UNIT)
-            zb = work.tile([P, UNIT, PACK], BF16, name="zb", align_bytes=64)
-            nc.scalar.copy(zb[:].rearrange("p (c i) t -> p c t i", i=4), z[:, :, u0 : u0 + UNIT].rearrange("p t (c i) -> p c t i", i=4))
-            nc.vector.quantize_mx(out=z_words[:, cols].bitcast(FP8X4), scales=z_scales[:, cols], in_=zb[:].rearrange("p j t -> p (j t)"))
+            def third(b, t):
+                nc.vector.tensor_tensor(excess[:, t, :], window(2, t, u), a[:, t, :], ALU.subtract)
+
+            best_of_two(u, third)
+            bank = turn(a, (u - 2) % 3)
+            room[u + 1] = new_room(u + 1)
+            best_t = room[u + 1][:, 2]
+            nc.scalar.copy(best_t, bank[:])
+            bank = turn(excess, (u - 1) % 3)
+            rise_t = tagged([P, PACK, P], F32, "rise_t", "rise%d" % u)
+            nc.scalar.activation(rise_t[:], bank[:], RELU)
+            add_turned(total, best_t, False, False)
+            add_turned(total, rise_t, False, True)
+            pairs = tagged([P, 2, UNIT, 2], BF16, "pairs", "pairs%d" % u)
+            for t in (0, 2, 1, 3):
+                nc.scalar.activation(pairs[:, t // 2, :, t % 2], total[:, t, :], COPY, scale=gain[:, t : t + 1])
+            zb = tagged([P, UNIT * PACK], BF16, "zb", "zb%d" % u)
+            nc.scalar.copy(zb[:].bitcast(F32).rearrange("p (j h) -> p j h", h=2),
+                           pairs[:].rearrange("p h j e -> p (h j e)").bitcast(F32).rearrange("p (h j) -> p j h", h=2))
+            return zb[:]
+
+        def score(zb, u):
+            cols = slice(u * UNIT, (u + 1) * UNIT)
+            nc.vector.quantize_mx(out=z_words[:, cols].bitcast(FP8X4), scales=z_scales[:, cols], in_=zb)
             bank = psum.tile([P, PACK, UNIT], F32, name="bank")
             for t in range(PACK):
                 rows = slice(t * P, (t + 1) * P)
                 nc.tensor.matmul_mx(out=bank[:, t, :], lhsT=cand_wd[:, rows].bitcast(FP8X4), lhsT_scale=cand_sd[:, rows],
                                     rhs=z_words[:, cols].bitcast(FP8X4), rhs_scale=z_scales[:, cols], start=True, stop=True)
-            ob = work.tile([P, UNIT, PACK], BF16, name="ob", align_bytes=64)
+            ob = tagged([P, UNIT, PACK], BF16, "ob", "ob%d" % u)
             nc.scalar.activation(ob[:], bank[:].rearrange("p t j -> p j t"), COPY, scale=0.0625)
             of = work.tile([P, PACK, UNIT], F32, name="of")
-            nc.scalar.activation(of[:], bank[:], COPY, scale=0.0625)
-            nc.sync.dma_start(out_rows[:, :, cols], of[:])
+            for rows in (slice(0, 2), slice(2, 4)) if u == UNITS - 1 else (slice(0, 4),):
+                nc.scalar.activation(of[:, rows, :], bank[:, rows, :], COPY, scale=0.0625)
+                (nc.scalar if rows.start else nc.sync).dma_start(out_rows[:, rows, cols], of[:, rows, :])
             nc.vector.quantize_mx(out=o_words[:, cols].bitcast(FP8X4), scales=o_scales[:, cols], in_=ob[:].rearrange("p j t -> p (j t)"))
             nc.sync.dma_start(out_words[:, cols], o_words[:, cols].bitcast(I32))
 
-        for j0, n in CHUNKS:
-            z = trellis(j0, n)
-            for u0 in range(0, n, UNIT):
-                score(z, j0, u0)
+        for u in range(UNITS - 1):
+            score(trellis(u), u)
+
+        bank = psum.tile([P, PACK, UNIT], F32, name="bank")
+        emit_last = held([P, PACK, UNIT], F32, "emit_last")
+        for t in range(PACK):
+            nc.tensor.transpose(bank[:, t, :], emit[UNITS - 1][:, t, :], ident[:])
+        for t in range(PACK):
+            nc.scalar.activation(emit_last[:, t, :], bank[:, t, :], COPY, scale=gain[:, t : t + 1])
+
+        u = UNITS - 1
+        a = room[u][:, 0]
+        z = held([P, PACK, UNIT], F32, "z")
+        late = tagged([P, 2, UNIT], F32, "late", "pairs%d" % (u - 1))
+        reach_c = []
+
+        def third_last(b, t):
+            reach_c.append(b[:, t, :] if t < 2 else late[:, t - 2, :])
+            nc.vector.tensor_copy(reach_c[t], window(2, t, u))
+
+        best_of_two(u, third_last)
+        zb = tagged([P, UNIT, PACK], BF16, "zb_last", "zb%d" % (u - 1))
+        for half in (slice(0, 2), slice(2, 4)):
+            for t in range(half.start, half.stop):
+                nc.vector.tensor_tensor(a[:, t, :], a[:, t, :], reach_c[t], ALU.max)
+            for t in range(half.start, half.stop):
+                nc.vector.scalar_tensor_tensor(z[:, t, :], a[:, t, :], gain[:, t : t + 1], emit_last[:, t, :], ALU.mult, ALU.add)
+        for half in (slice(0, 2), slice(2, 4)):
+            nc.vector.tensor_copy(zb[:, :, half].rearrange("p (c i) t -> p c t i", i=4), z[:, half, :].rearrange("p t (c i) -> p c t i", i=4))
+        score(zb[:].rearrange("p j t -> p (j t)"), u)
         for q in range(4):
-            nc.sync.dma_start(out_2[0, 4 * q : 4 * q + 4, :].bitcast(I32), o_scales[32 * q : 32 * q + 4, :].bitcast(I32))
+            (nc.sync if q < 2 else nc.scalar).dma_start(out_2[0, 4 * q : 4 * q + 4, :].bitcast(I32), o_scales[32 * q : 32 * q + 4, :].bitcast(I32))

@@ -12,7 +12,6 @@ U8 = mybir.dt.uint8
 FP8X4 = mybir.dt.float8_e4m3fn_x4
 ALU = mybir.AluOpType
 COPY = mybir.ActivationFunctionType.Copy
-IDENTITY = mybir.ActivationFunctionType.Identity
 RELU = mybir.ActivationFunctionType.Relu
 
 P = 128
@@ -57,8 +56,10 @@ def tile_picked_viterb3_none_po_kernel(tc, x_words, x_scales, w1_words, w1_scale
         xw = held([P, T], U32, "xw")
         xs = held([P, T], U8, "xs")
         w1_raw, w2_raw = held([P, S], U32, "w1_raw"), held([P, S], U32, "w2_raw")
-        w1s_raw, w2s_raw = held([P, S], U8, "w1s_raw"), held([P, S], U8, "w2s_raw")
-        tr_rows = held([P, P], F32, "tr_rows")
+        w1s_raw, w2s_raw = tagged([P, S], U8, "w1s_raw", "w1s_raw"), held([P, S], U8, "w2s_raw")
+        lead = [held([P, S], F32, "tr1_all"), held([P, S], F32, "tr2_all")]
+        tr3_rows = held([P, P], F32, "tr3_rows")
+        tr3_last = held([P, UNIT], F32, "tr3_last")
         gain = held([P, PACK], F32, "gain")
 
         def load_scales(tile, scales):
@@ -67,8 +68,8 @@ def tile_picked_viterb3_none_po_kernel(tc, x_words, x_scales, w1_words, w1_scale
 
         nc.gpsimd.memset(xs[:].bitcast(I32), 0)
         nc.vector.memset(w1s_raw[:].bitcast(I32), 0)
-        nc.vector.memset(tr_rows[:], 0.0)
         nc.vector.memset(w2s_raw[:].bitcast(I32), 0)
+        nc.vector.memset(tr3_rows[:], 0.0)
         ident = held([P, P], F32, "ident")
         make_identity(nc, ident[:])
         nc.sync.dma_start(w1_raw[:].bitcast(I32), words_of(w1_words))
@@ -76,18 +77,20 @@ def tile_picked_viterb3_none_po_kernel(tc, x_words, x_scales, w1_words, w1_scale
         nc.sync.dma_start(offs_l[:], offs)
         nc.sync.dma_start(two_l[:], two)
         nc.sync.dma_start(xw[:].bitcast(I32), words_of(x_words))
-        for k, scores in enumerate((tr1, tr2, tr3)):
-            nc.sync.dma_start(tr_rows[UNITS * k : UNITS * (k + 1), :], scores[0:1, :].rearrange("o (u j) -> (o u) j", j=UNIT))
         load_scales(w1s_raw, w1_scales)
         nc.sync.dma_start(cand_l[:], cand)
-        nc.sync.dma_start(s_l[0][:], s1)
         nc.sync.dma_start(w2_raw[:].bitcast(I32), words_of(w2_words))
+        nc.sync.dma_start(s_l[0][:], s1)
+        nc.sync.dma_start(lead[0][:], tr1)
         load_scales(w2s_raw, w2_scales)
         nc.sync.dma_start(s_l[1][:], s2)
+        nc.sync.dma_start(lead[1][:], tr2)
         nc.sync.dma_start(s_l[2][:], s3)
         nc.sync.dma_start(gain[:], gs.rearrange("(p t) o -> p (t o)", t=PACK))
+        nc.sync.dma_start(tr3_rows[0:UNITS, :], tr3[0:1, :].rearrange("o (u j) -> (o u) j", j=UNIT))
+        nc.sync.dma_start(tr3_last[:], tr3[:, S - UNIT : S])
 
-        offs_w, two_w, cand_w = held([P, S], U32, "offs_w"), held([P, S], U32, "two_w"), held([P, S], U32, "cand_w")
+        offs_w = held([P, S], U32, "offs_w")
         offs_s, two_s, cand_s = held([P, S], U8, "offs_s"), held([P, S], U8, "two_s"), held([P, S], U8, "cand_s")
         w1_dealt = held([P, S], U32, "w1_dealt")
         w1s_dealt = held([P, S], U8, "w1s_dealt")
@@ -99,25 +102,8 @@ def tile_picked_viterb3_none_po_kernel(tc, x_words, x_scales, w1_words, w1_scale
         nc.vector.tensor_copy(two_s[:], xs[:].indirect(two_l[:]))
         nc.vector.tensor_copy(offs_w[:], xw[:].indirect(offs_l[:]))
         nc.vector.tensor_copy(dealt(w1s_dealt[:]), plain(w1s_raw[:]))
+        two_w = tagged([P, S], U32, "two_w", "w1s_raw")
         nc.vector.tensor_copy(two_w[:], xw[:].indirect(two_l[:]))
-
-        bank = turns.tile([P, P], F32, name="turn", tag="turn0")
-        nc.tensor.transpose(bank[:], tr_rows[:], ident[:])
-        last_cols = held([P, UNITS], F32, "last_cols")
-        minus_last = held([P, UNITS], F32, "minus_last")
-        lead_cols = held([P, 2 * UNITS], F32, "lead_cols")
-        nc.scalar.activation(minus_last[:], bank[:, 2 * UNITS : 3 * UNITS], COPY, scale=-1.0)
-        nc.scalar.copy(last_cols[:], bank[:, 2 * UNITS : 3 * UNITS])
-        for u in range(UNITS):
-            nc.scalar.activation(lead_cols[:, u : 2 * UNITS : UNITS], bank[:, u : 2 * UNITS : UNITS], IDENTITY, bias=minus_last[:, u : u + 1])
-        lead = []
-        for k in range(2):
-            bank = turns.tile([P, S], F32, name="turn", tag="turn%d" % (k + 1))
-            for u in range(UNITS):
-                column = lead_cols[:, UNITS * k + u : UNITS * k + u + 1]
-                nc.tensor.transpose(bank[:, u * UNIT : (u + 1) * UNIT], column.to_broadcast([P, P]), ident[:])
-            lead.append(held([P, S], F32, "lead%d" % k))
-            nc.scalar.copy(lead[k][:], bank[:])
 
         y = [held([P, S], F32, "y%d" % t) for t in range(PACK)]
         for t in range(PACK):
@@ -127,19 +113,29 @@ def tile_picked_viterb3_none_po_kernel(tc, x_words, x_scales, w1_words, w1_scale
                                 rhs=offs_w[:].bitcast(FP8X4), rhs_scale=offs_s[:], start=True, stop=True)
             nc.scalar.copy(y[t][:], bank[:])
 
-        emit = []
-        for u in range(UNITS):
+        emit = {}
+        for u in (UNITS - 1, 0, 1, 2):
             cols = slice(u * UNIT, (u + 1) * UNIT)
             bank = psum.tile([P, S], F32, name="bank")
             nc.tensor.matmul_mx(out=bank[:], lhsT=two_w[:, cols].bitcast(FP8X4), lhsT_scale=two_s[:, cols],
                                 rhs=w2_raw[:].bitcast(FP8X4), rhs_scale=w2s_raw[:], start=True, stop=True)
-            emit.append(held([P, PACK, P], F32, "emit%d" % u))
-            nc.scalar.activation(emit[u][:], bank[:].rearrange("j (p t) -> j t p", t=PACK), IDENTITY, bias=last_cols[:, u : u + 1])
+            emit[u] = held([P, PACK, P], F32, "emit%d" % u)
+            nc.scalar.copy(emit[u][:], bank[:].rearrange("j (p t) -> j t p", t=PACK))
 
         nc.vector.tensor_copy(cand_s[:], xs[:].indirect(cand_l[:]))
-        nc.vector.tensor_copy(cand_w[:], xw[:].indirect(cand_l[:]))
         nc.vector.tensor_copy(dealt(cand_sd[:]), plain(cand_s[:]))
-        nc.vector.tensor_copy(dealt(cand_wd[:]), plain(cand_w[:]))
+
+        bank = psum.tile([P, P], F32, name="bank")
+        nc.tensor.transpose(bank[:], tr3_rows[:], ident[:])
+        tr3_cols = held([P, UNITS], F32, "tr3_cols")
+        nc.scalar.copy(tr3_cols[:], bank[:, 0:UNITS])
+
+        bank = psum.tile([P, PACK, UNIT], F32, name="bank")
+        emit_last = held([P, PACK, UNIT], F32, "emit_last")
+        for t in range(PACK):
+            nc.tensor.transpose(bank[:, t, :], emit[UNITS - 1][:, t, :], ident[:])
+        for t in range(PACK):
+            nc.scalar.activation(emit_last[:, t, :], bank[:, t, :], COPY, scale=gain[:, t : t + 1])
 
         z_words = held([P, S], U32, "z_words")
         z_scales = held([P, S], U8, "z_scales")
@@ -156,9 +152,14 @@ def tile_picked_viterb3_none_po_kernel(tc, x_words, x_scales, w1_words, w1_scale
 
         room = {0: new_room(0)}
 
+        first_0 = held([P, PACK, UNIT], F32, "first_0")
+
+        def first(u):
+            return room[u][:, 0] if u else first_0[:]
+
         def best_of_two(u, then):
             cols = slice(u * UNIT, (u + 1) * UNIT)
-            a, b = room[u][:, 0], room[u][:, 1]
+            a, b = first(u), room[u][:, 1]
             for t in range(PACK):
                 nc.vector.tensor_tensor(a[:, t, :], window(0, t, u), lead[0][:, cols], ALU.add)
             for t in range(PACK):
@@ -184,7 +185,7 @@ def tile_picked_viterb3_none_po_kernel(tc, x_words, x_scales, w1_words, w1_scale
             total = turns.tile([P, PACK, UNIT], F32, name="total", tag="turn%d" % (u % 3))
             add_turned(total, emit[u], True, False)
             excess = tagged([P, PACK, UNIT], F32, "excess", "excess%d" % u)
-            a = room[u][:, 0]
+            a = first(u)
 
             def third(b, t):
                 nc.vector.tensor_tensor(excess[:, t, :], window(2, t, u), a[:, t, :], ALU.subtract)
@@ -192,11 +193,11 @@ def tile_picked_viterb3_none_po_kernel(tc, x_words, x_scales, w1_words, w1_scale
             best_of_two(u, third)
             bank = turn(a, (u - 2) % 3)
             room[u + 1] = new_room(u + 1)
-            best_t = room[u + 1][:, 2]
+            best_t = room[u + 1][:, 2] if u else held([P, PACK, P], F32, "best_first")[:]
             nc.scalar.copy(best_t, bank[:])
             bank = turn(excess, (u - 1) % 3)
             rise_t = tagged([P, PACK, P], F32, "rise_t", "rise%d" % u)
-            nc.scalar.activation(rise_t[:], bank[:], RELU)
+            nc.scalar.activation(rise_t[:], bank[:], RELU, bias=tr3_cols[:, u : u + 1])
             add_turned(total, best_t, False, False)
             add_turned(total, rise_t, False, True)
             pairs = tagged([P, 2, UNIT, 2], BF16, "pairs", "pairs%d" % u)
@@ -225,14 +226,12 @@ def tile_picked_viterb3_none_po_kernel(tc, x_words, x_scales, w1_words, w1_scale
             nc.sync.dma_start(out_words[:, cols], o_words[:, cols].bitcast(I32))
 
         for u in range(UNITS - 1):
-            score(trellis(u), u)
-
-        bank = psum.tile([P, PACK, UNIT], F32, name="bank")
-        emit_last = held([P, PACK, UNIT], F32, "emit_last")
-        for t in range(PACK):
-            nc.tensor.transpose(bank[:, t, :], emit[UNITS - 1][:, t, :], ident[:])
-        for t in range(PACK):
-            nc.scalar.activation(emit_last[:, t, :], bank[:, t, :], COPY, scale=gain[:, t : t + 1])
+            zb = trellis(u)
+            if u == 0:
+                cand_w = tagged([P, S], U32, "cand_w", "rise0")
+                nc.vector.tensor_copy(cand_w[:], xw[:].indirect(cand_l[:]))
+                nc.vector.tensor_copy(dealt(cand_wd[:]), plain(cand_w[:]))
+            score(zb, u)
 
         u = UNITS - 1
         a = room[u][:, 0]
@@ -242,7 +241,7 @@ def tile_picked_viterb3_none_po_kernel(tc, x_words, x_scales, w1_words, w1_scale
 
         def third_last(b, t):
             reach_c.append(b[:, t, :] if t < 2 else late[:, t - 2, :])
-            nc.vector.tensor_copy(reach_c[t], window(2, t, u))
+            nc.vector.tensor_tensor(reach_c[t], window(2, t, u), tr3_last[:], ALU.add)
 
         best_of_two(u, third_last)
         zb = tagged([P, UNIT, PACK], BF16, "zb_last", "zb%d" % (u - 1))

@@ -18,8 +18,15 @@ P = 128
 PACK = 4
 T = 2048
 S = 512
+GROUP = 16
+QUADRANTS = 4
 UNIT = 128
 UNITS = S // UNIT
+LAST = UNITS - 1
+TURN_BANKS = 3
+PRODUCT_BANKS = 8 - TURN_BANKS
+HALVES = (slice(0, 2), slice(2, 4))
+OUT_SCALE = 0.0625
 FLOPS = 3 * 2 * 512 * 512 * 512
 
 
@@ -29,229 +36,233 @@ def tile_picked_viterb3_none_po_kernel(tc, x_words, x_scales, w1_words, w1_scale
     def words_of(ap):
         return ap[0].rearrange("p n t -> p (n t)").bitcast(I32)
 
-    def dealt(ap):
-        return ap.rearrange("p (t m) -> p m t", t=PACK)
+    def deal(dst, src):
+        nc.vector.tensor_copy(dst[:].rearrange("p (t m) -> p m t", t=PACK), src[:].rearrange("p (m t) -> p m t", t=PACK))
 
-    def plain(ap):
-        return ap.rearrange("p (m t) -> p m t", t=PACK)
+    def places(u):
+        return slice(u * UNIT, (u + 1) * UNIT)
 
     with ExitStack() as ctx:
         lists = ctx.enter_context(tc.tile_pool(name="lists", bufs=1))
         keep = ctx.enter_context(tc.tile_pool(name="keep", bufs=1))
-        work = ctx.enter_context(tc.tile_pool(name="work", bufs=2))
-        psum = ctx.enter_context(tc.psum_pool(name="psum", bufs=5))
+        stage = ctx.enter_context(tc.tile_pool(name="stage", bufs=2))
+        products = ctx.enter_context(tc.psum_pool(name="products", bufs=PRODUCT_BANKS))
         turns = ctx.enter_context(tc.psum_pool(name="turns", bufs=1))
 
         def new_list(name):
-            return lists.tile([P, S // 16], U16, name=name)
+            return lists.tile([P, S // GROUP], U16, name=name)
 
         def held(shape, dtype, name):
             return keep.tile(shape, dtype, name=name, align_bytes=64)
 
-        def tagged(shape, dtype, name, tag):
+        def in_place_of(tag, shape, dtype, name):
             return keep.tile(shape, dtype, name=name, tag=tag, align_bytes=64)
 
-        offs_l, two_l, cand_l = new_list("offs_l"), new_list("two_l"), new_list("cand_l")
-        s_l = [new_list("s1_l"), new_list("s2_l"), new_list("s3_l")]
-        xw = held([P, T], U32, "xw")
-        xs = held([P, T], U8, "xs")
-        w1_raw, w2_raw = held([P, S], U32, "w1_raw"), held([P, S], U32, "w2_raw")
-        w1s_raw, w2s_raw = tagged([P, S], U8, "w1s_raw", "w1s_raw"), held([P, S], U8, "w2s_raw")
-        lead = [held([P, S], F32, "tr1_all"), held([P, S], F32, "tr2_all")]
+        offs_list, two_list, cand_list = new_list("offs_list"), new_list("two_list"), new_list("cand_list")
+        source_lists = [new_list("s1_list"), new_list("s2_list"), new_list("s3_list")]
+        x_w = held([P, T], U32, "x_w")
+        x_s = held([P, T], U8, "x_s")
+        w1_w, w2_w = held([P, S], U32, "w1_w"), held([P, S], U32, "w2_w")
+        w1_s, w2_s = in_place_of("w1_s", [P, S], U8, "w1_s"), held([P, S], U8, "w2_s")
+        tr1_all, tr2_all = held([P, S], F32, "tr1_all"), held([P, S], F32, "tr2_all")
         tr3_rows = held([P, P], F32, "tr3_rows")
         tr3_last = held([P, UNIT], F32, "tr3_last")
         gain = held([P, PACK], F32, "gain")
 
         def load_scales(tile, scales):
-            for q in range(4):
+            for q in range(QUADRANTS):
                 nc.sync.dma_start(tile[32 * q : 32 * q + 4, :].bitcast(I32), scales[0, 4 * q : 4 * q + 4, :].bitcast(I32))
 
-        nc.gpsimd.memset(xs[:].bitcast(I32), 0)
-        nc.vector.memset(w1s_raw[:].bitcast(I32), 0)
-        nc.vector.memset(w2s_raw[:].bitcast(I32), 0)
+        nc.gpsimd.memset(x_s[:].bitcast(I32), 0)
+        nc.vector.memset(w1_s[:].bitcast(I32), 0)
+        nc.vector.memset(w2_s[:].bitcast(I32), 0)
         nc.vector.memset(tr3_rows[:], 0.0)
         ident = held([P, P], F32, "ident")
         make_identity(nc, ident[:])
-        nc.sync.dma_start(w1_raw[:].bitcast(I32), words_of(w1_words))
-        load_scales(xs, x_scales)
-        nc.sync.dma_start(offs_l[:], offs)
-        nc.sync.dma_start(two_l[:], two)
-        nc.sync.dma_start(xw[:].bitcast(I32), words_of(x_words))
-        load_scales(w1s_raw, w1_scales)
-        nc.sync.dma_start(cand_l[:], cand)
-        nc.sync.dma_start(w2_raw[:].bitcast(I32), words_of(w2_words))
-        nc.sync.dma_start(s_l[0][:], s1)
-        nc.sync.dma_start(lead[0][:], tr1)
-        load_scales(w2s_raw, w2_scales)
-        nc.sync.dma_start(s_l[1][:], s2)
-        nc.sync.dma_start(lead[1][:], tr2)
-        nc.sync.dma_start(s_l[2][:], s3)
+
+        nc.sync.dma_start(w1_w[:].bitcast(I32), words_of(w1_words))
+        load_scales(x_s, x_scales)
+        nc.sync.dma_start(offs_list[:], offs)
+        nc.sync.dma_start(two_list[:], two)
+        nc.sync.dma_start(x_w[:].bitcast(I32), words_of(x_words))
+        load_scales(w1_s, w1_scales)
+        nc.sync.dma_start(cand_list[:], cand)
+        nc.sync.dma_start(w2_w[:].bitcast(I32), words_of(w2_words))
+        nc.sync.dma_start(source_lists[0][:], s1)
+        nc.sync.dma_start(tr1_all[:], tr1)
+        load_scales(w2_s, w2_scales)
+        nc.sync.dma_start(source_lists[1][:], s2)
+        nc.sync.dma_start(tr2_all[:], tr2)
+        nc.sync.dma_start(source_lists[2][:], s3)
         nc.sync.dma_start(gain[:], gs.rearrange("(p t) o -> p (t o)", t=PACK))
-        nc.sync.dma_start(tr3_rows[0:UNITS, :], tr3[0:1, :].rearrange("o (u j) -> (o u) j", j=UNIT))
-        nc.sync.dma_start(tr3_last[:], tr3[:, S - UNIT : S])
+        nc.sync.dma_start(tr3_rows[0:LAST, :], tr3[0:1, 0 : LAST * UNIT].rearrange("o (u j) -> (o u) j", j=UNIT))
+        nc.sync.dma_start(tr3_last[:], tr3[:, places(LAST)])
 
         offs_w = held([P, S], U32, "offs_w")
         offs_s, two_s, cand_s = held([P, S], U8, "offs_s"), held([P, S], U8, "two_s"), held([P, S], U8, "cand_s")
-        w1_dealt = held([P, S], U32, "w1_dealt")
-        w1s_dealt = held([P, S], U8, "w1s_dealt")
-        cand_wd = held([P, S], U32, "cand_wd")
-        cand_sd = held([P, S], U8, "cand_sd")
+        w1_w_dealt = held([P, S], U32, "w1_w_dealt")
+        w1_s_dealt = held([P, S], U8, "w1_s_dealt")
+        cand_w_dealt = held([P, S], U32, "cand_w_dealt")
+        cand_s_dealt = held([P, S], U8, "cand_s_dealt")
 
-        nc.vector.tensor_copy(dealt(w1_dealt[:]), plain(w1_raw[:]))
-        nc.vector.tensor_copy(offs_s[:], xs[:].indirect(offs_l[:]))
-        nc.vector.tensor_copy(two_s[:], xs[:].indirect(two_l[:]))
-        nc.vector.tensor_copy(offs_w[:], xw[:].indirect(offs_l[:]))
-        nc.vector.tensor_copy(dealt(w1s_dealt[:]), plain(w1s_raw[:]))
-        two_w = tagged([P, S], U32, "two_w", "w1s_raw")
-        nc.vector.tensor_copy(two_w[:], xw[:].indirect(two_l[:]))
+        deal(w1_w_dealt, w1_w)
+        nc.vector.tensor_copy(offs_s[:], x_s[:].indirect(offs_list[:]))
+        nc.vector.tensor_copy(two_s[:], x_s[:].indirect(two_list[:]))
+        nc.vector.tensor_copy(offs_w[:], x_w[:].indirect(offs_list[:]))
+        deal(w1_s_dealt, w1_s)
+        two_w = in_place_of("w1_s", [P, S], U32, "two_w")
+        nc.vector.tensor_copy(two_w[:], x_w[:].indirect(two_list[:]))
 
         y = [held([P, S], F32, "y%d" % t) for t in range(PACK)]
         for t in range(PACK):
-            cols = slice(t * P, (t + 1) * P)
-            bank = psum.tile([P, S], F32, name="bank")
-            nc.tensor.matmul_mx(out=bank[:], lhsT=w1_dealt[:, cols].bitcast(FP8X4), lhsT_scale=w1s_dealt[:, cols],
+            dealt = slice(t * P, (t + 1) * P)
+            bank = products.tile([P, S], F32, name="bank")
+            nc.tensor.matmul_mx(out=bank[:], lhsT=w1_w_dealt[:, dealt].bitcast(FP8X4), lhsT_scale=w1_s_dealt[:, dealt],
                                 rhs=offs_w[:].bitcast(FP8X4), rhs_scale=offs_s[:], start=True, stop=True)
             nc.scalar.copy(y[t][:], bank[:])
 
-        emit = {}
-        for u in (UNITS - 1, 0, 1, 2):
-            cols = slice(u * UNIT, (u + 1) * UNIT)
-            bank = psum.tile([P, S], F32, name="bank")
-            nc.tensor.matmul_mx(out=bank[:], lhsT=two_w[:, cols].bitcast(FP8X4), lhsT_scale=two_s[:, cols],
-                                rhs=w2_raw[:].bitcast(FP8X4), rhs_scale=w2s_raw[:], start=True, stop=True)
-            emit[u] = held([P, PACK, P], F32, "emit%d" % u)
-            nc.scalar.copy(emit[u][:], bank[:].rearrange("j (p t) -> j t p", t=PACK))
+        c_turned = {}
+        for u in [LAST] + list(range(LAST)):
+            bank = products.tile([P, S], F32, name="bank")
+            nc.tensor.matmul_mx(out=bank[:], lhsT=two_w[:, places(u)].bitcast(FP8X4), lhsT_scale=two_s[:, places(u)],
+                                rhs=w2_w[:].bitcast(FP8X4), rhs_scale=w2_s[:], start=True, stop=True)
+            c_turned[u] = held([P, PACK, P], F32, "c_turned%d" % u)
+            nc.scalar.copy(c_turned[u][:], bank[:].rearrange("j (p t) -> j t p", t=PACK))
 
-        nc.vector.tensor_copy(cand_s[:], xs[:].indirect(cand_l[:]))
-        nc.vector.tensor_copy(dealt(cand_sd[:]), plain(cand_s[:]))
+        nc.vector.tensor_copy(cand_s[:], x_s[:].indirect(cand_list[:]))
+        deal(cand_s_dealt, cand_s)
 
-        bank = psum.tile([P, P], F32, name="bank")
+        bank = products.tile([P, P], F32, name="bank")
         nc.tensor.transpose(bank[:], tr3_rows[:], ident[:])
-        tr3_cols = held([P, UNITS], F32, "tr3_cols")
-        nc.scalar.copy(tr3_cols[:], bank[:, 0:UNITS])
+        tr3_cols = held([P, LAST], F32, "tr3_cols")
+        nc.scalar.copy(tr3_cols[:], bank[:, 0:LAST])
 
-        bank = psum.tile([P, PACK, UNIT], F32, name="bank")
-        emit_last = held([P, PACK, UNIT], F32, "emit_last")
+        bank = products.tile([P, PACK, UNIT], F32, name="bank")
+        weighted_c_last = held([P, PACK, UNIT], F32, "weighted_c_last")
         for t in range(PACK):
-            nc.tensor.transpose(bank[:, t, :], emit[UNITS - 1][:, t, :], ident[:])
+            nc.tensor.transpose(bank[:, t, :], c_turned[LAST][:, t, :], ident[:])
         for t in range(PACK):
-            nc.scalar.activation(emit_last[:, t, :], bank[:, t, :], COPY, scale=gain[:, t : t + 1])
+            nc.scalar.activation(weighted_c_last[:, t, :], bank[:, t, :], COPY, scale=gain[:, t : t + 1])
 
-        z_words = held([P, S], U32, "z_words")
-        z_scales = held([P, S], U8, "z_scales")
-        o_words = held([P, S], U32, "o_words")
-        o_scales = held([P, S], U8, "o_scales")
-        out_rows = out_0.rearrange("(p t) j -> p t j", t=PACK)
+        z_w = held([P, S], U32, "z_w")
+        z_s = held([P, S], U8, "z_s")
+        out_w = held([P, S], U32, "out_w")
+        out_s = held([P, S], U8, "out_s")
+        out_planes = out_0.rearrange("(p t) j -> p t j", t=PACK)
         out_words = words_of(out_1)
 
-        def window(k, t, u):
-            return y[t][:].indirect(s_l[k][:, u * UNIT // 16 : (u + 1) * UNIT // 16])
+        def looked_up(k, t, u):
+            return y[t][:].indirect(source_lists[k][:, u * UNIT // GROUP : (u + 1) * UNIT // GROUP])
 
         def new_room(u):
-            return tagged([P, 3, PACK, UNIT], F32, "room", "pairs%d" % max(u - 2, -1))
+            return in_place_of("pairs%d" % max(u - 2, -1), [P, 3, PACK, UNIT], F32, "room")
 
         room = {0: new_room(0)}
+        best_0 = held([P, PACK, UNIT], F32, "best_0")
 
-        first_0 = held([P, PACK, UNIT], F32, "first_0")
+        def best_tile(u):
+            return room[u][:, 0] if u else best_0[:]
 
-        def first(u):
-            return room[u][:, 0] if u else first_0[:]
-
-        def best_of_two(u, then):
-            cols = slice(u * UNIT, (u + 1) * UNIT)
-            a, b = first(u), room[u][:, 1]
+        def best_of_two(u, third):
+            best, second = best_tile(u), room[u][:, 1]
+            low, high = HALVES
             for t in range(PACK):
-                nc.vector.tensor_tensor(a[:, t, :], window(0, t, u), lead[0][:, cols], ALU.add)
-            for t in range(PACK):
-                if t == PACK - 1:
-                    nc.vector.tensor_tensor(a[:, 0:2, :], a[:, 0:2, :], b[:, 0:2, :], ALU.max)
-                nc.vector.tensor_tensor(b[:, t, :], window(1, t, u), lead[1][:, cols], ALU.add)
-            then(b, 0)
-            nc.vector.tensor_tensor(a[:, 2:4, :], a[:, 2:4, :], b[:, 2:4, :], ALU.max)
+                nc.vector.tensor_tensor(best[:, t, :], looked_up(0, t, u), tr1_all[:, places(u)], ALU.add)
+            for t in range(PACK - 1):
+                nc.vector.tensor_tensor(second[:, t, :], looked_up(1, t, u), tr2_all[:, places(u)], ALU.add)
+            nc.vector.tensor_tensor(best[:, low, :], best[:, low, :], second[:, low, :], ALU.max)
+            nc.vector.tensor_tensor(second[:, PACK - 1, :], looked_up(1, PACK - 1, u), tr2_all[:, places(u)], ALU.add)
+            third(0)
+            nc.vector.tensor_tensor(best[:, high, :], best[:, high, :], second[:, high, :], ALU.max)
             for t in range(1, PACK):
-                then(b, t)
+                third(t)
 
-        def turn(src, side):
-            bank = turns.tile([P, PACK, P], F32, name="turn", tag="turn%d" % side)
+        def turn_bank(number):
+            return turns.tile([P, PACK, P], F32, name="turn", tag="turn%d" % (number % TURN_BANKS))
+
+        def turn(planes, number):
+            bank = turn_bank(number)
             for t in range(PACK):
-                nc.tensor.transpose(bank[:, t, :], src[:, t, :], ident[:])
+                nc.tensor.transpose(bank[:, t, :], planes[:, t, :], ident[:])
             return bank
 
-        def add_turned(total, term, opens, closes):
+        def add_turned_back(total, term, opens, closes):
             for t in range(PACK):
                 nc.tensor.matmul(total[:, t, :], term[:, t, :], ident[:], start=(opens and t == 0), stop=(closes and t == PACK - 1), is_transpose=True)
 
-        def trellis(u):
-            total = turns.tile([P, PACK, UNIT], F32, name="total", tag="turn%d" % (u % 3))
-            add_turned(total, emit[u], True, False)
-            excess = tagged([P, PACK, UNIT], F32, "excess", "excess%d" % u)
-            a = first(u)
+        def rounded_z(u):
+            total = turn_bank(u)
+            add_turned_back(total, c_turned[u], True, False)
+            excess = held([P, PACK, UNIT], F32, "excess%d" % u)
+            best = best_tile(u)
 
-            def third(b, t):
-                nc.vector.tensor_tensor(excess[:, t, :], window(2, t, u), a[:, t, :], ALU.subtract)
+            def third(t):
+                nc.vector.tensor_tensor(excess[:, t, :], looked_up(2, t, u), best[:, t, :], ALU.subtract)
 
             best_of_two(u, third)
-            bank = turn(a, (u - 2) % 3)
+            bank = turn(best, u - 2)
             room[u + 1] = new_room(u + 1)
-            best_t = room[u + 1][:, 2] if u else held([P, PACK, P], F32, "best_first")[:]
-            nc.scalar.copy(best_t, bank[:])
-            bank = turn(excess, (u - 1) % 3)
-            rise_t = tagged([P, PACK, P], F32, "rise_t", "rise%d" % u)
-            nc.scalar.activation(rise_t[:], bank[:], RELU, bias=tr3_cols[:, u : u + 1])
-            add_turned(total, best_t, False, False)
-            add_turned(total, rise_t, False, True)
-            pairs = tagged([P, 2, UNIT, 2], BF16, "pairs", "pairs%d" % u)
-            for t in (0, 2, 1, 3):
-                nc.scalar.activation(pairs[:, t // 2, :, t % 2], total[:, t, :], COPY, scale=gain[:, t : t + 1])
-            zb = tagged([P, UNIT * PACK], BF16, "zb", "zb%d" % u)
-            nc.scalar.copy(zb[:].bitcast(F32).rearrange("p (j h) -> p j h", h=2),
+            best_turned = room[u + 1][:, 2] if u else held([P, PACK, P], F32, "best_turned_0")[:]
+            nc.scalar.copy(best_turned, bank[:])
+            bank = turn(excess, u - 1)
+            rise_turned = in_place_of("rise%d" % u, [P, PACK, P], F32, "rise_turned")
+            nc.scalar.activation(rise_turned[:], bank[:], RELU, bias=tr3_cols[:, u : u + 1])
+            add_turned_back(total, best_turned, False, False)
+            add_turned_back(total, rise_turned, False, True)
+            pairs = in_place_of("pairs%d" % u, [P, 2, UNIT, 2], BF16, "pairs")
+            for e in range(2):
+                for h in range(2):
+                    t = 2 * h + e
+                    nc.scalar.activation(pairs[:, h, :, e], total[:, t, :], COPY, scale=gain[:, t : t + 1])
+            z_bf = in_place_of("z_bf%d" % u, [P, UNIT * PACK], BF16, "z_bf")
+            nc.scalar.copy(z_bf[:].bitcast(F32).rearrange("p (j h) -> p j h", h=2),
                            pairs[:].rearrange("p h j e -> p (h j e)").bitcast(F32).rearrange("p (h j) -> p j h", h=2))
-            return zb[:]
+            return z_bf[:]
 
-        def score(zb, u):
-            cols = slice(u * UNIT, (u + 1) * UNIT)
-            nc.vector.quantize_mx(out=z_words[:, cols].bitcast(FP8X4), scales=z_scales[:, cols], in_=zb)
-            bank = psum.tile([P, PACK, UNIT], F32, name="bank")
+        def score(z_bf, u):
+            cols = places(u)
+            nc.vector.quantize_mx(out=z_w[:, cols].bitcast(FP8X4), scales=z_s[:, cols], in_=z_bf)
+            bank = products.tile([P, PACK, UNIT], F32, name="bank")
             for t in range(PACK):
-                rows = slice(t * P, (t + 1) * P)
-                nc.tensor.matmul_mx(out=bank[:, t, :], lhsT=cand_wd[:, rows].bitcast(FP8X4), lhsT_scale=cand_sd[:, rows],
-                                    rhs=z_words[:, cols].bitcast(FP8X4), rhs_scale=z_scales[:, cols], start=True, stop=True)
-            ob = tagged([P, UNIT, PACK], BF16, "ob", "ob%d" % u)
-            nc.scalar.activation(ob[:], bank[:].rearrange("p t j -> p j t"), COPY, scale=0.0625)
-            of = work.tile([P, PACK, UNIT], F32, name="of")
-            for rows in (slice(0, 2), slice(2, 4)) if u == UNITS - 1 else (slice(0, 4),):
-                nc.scalar.activation(of[:, rows, :], bank[:, rows, :], COPY, scale=0.0625)
-                (nc.scalar if rows.start else nc.sync).dma_start(out_rows[:, rows, cols], of[:, rows, :])
-            nc.vector.quantize_mx(out=o_words[:, cols].bitcast(FP8X4), scales=o_scales[:, cols], in_=ob[:].rearrange("p j t -> p (j t)"))
-            nc.sync.dma_start(out_words[:, cols], o_words[:, cols].bitcast(I32))
+                dealt = slice(t * P, (t + 1) * P)
+                nc.tensor.matmul_mx(out=bank[:, t, :], lhsT=cand_w_dealt[:, dealt].bitcast(FP8X4), lhsT_scale=cand_s_dealt[:, dealt],
+                                    rhs=z_w[:, cols].bitcast(FP8X4), rhs_scale=z_s[:, cols], start=True, stop=True)
+            out_bf = held([P, UNIT, PACK], BF16, "out_bf%d" % u)
+            nc.scalar.activation(out_bf[:], bank[:].rearrange("p t j -> p j t"), COPY, scale=OUT_SCALE)
+            out_f32 = stage.tile([P, PACK, UNIT], F32, name="out_f32")
+            pieces = ((nc.sync, HALVES[0]), (nc.scalar, HALVES[1])) if u == LAST else ((nc.sync, slice(0, PACK)),)
+            for queue, planes in pieces:
+                nc.scalar.activation(out_f32[:, planes, :], bank[:, planes, :], COPY, scale=OUT_SCALE)
+                queue.dma_start(out_planes[:, planes, cols], out_f32[:, planes, :])
+            nc.vector.quantize_mx(out=out_w[:, cols].bitcast(FP8X4), scales=out_s[:, cols], in_=out_bf[:].rearrange("p j t -> p (j t)"))
+            nc.sync.dma_start(out_words[:, cols], out_w[:, cols].bitcast(I32))
 
-        for u in range(UNITS - 1):
-            zb = trellis(u)
-            if u == 0:
-                cand_w = tagged([P, S], U32, "cand_w", "rise0")
-                nc.vector.tensor_copy(cand_w[:], xw[:].indirect(cand_l[:]))
-                nc.vector.tensor_copy(dealt(cand_wd[:]), plain(cand_w[:]))
-            score(zb, u)
+        z_bf_0 = rounded_z(0)
+        cand_w = in_place_of("rise0", [P, S], U32, "cand_w")
+        nc.vector.tensor_copy(cand_w[:], x_w[:].indirect(cand_list[:]))
+        deal(cand_w_dealt, cand_w)
+        score(z_bf_0, 0)
+        for u in range(1, LAST):
+            score(rounded_z(u), u)
 
-        u = UNITS - 1
-        a = room[u][:, 0]
-        z = held([P, PACK, UNIT], F32, "z")
-        late = tagged([P, 2, UNIT], F32, "late", "pairs%d" % (u - 1))
-        reach_c = []
+        best = best_tile(LAST)
+        z_last = held([P, PACK, UNIT], F32, "z_last")
+        late = in_place_of("pairs%d" % (LAST - 1), [P, 2, UNIT], F32, "late")
+        third_source = [room[LAST][:, 1, 0, :], room[LAST][:, 1, 1, :], late[:, 0, :], late[:, 1, :]]
 
-        def third_last(b, t):
-            reach_c.append(b[:, t, :] if t < 2 else late[:, t - 2, :])
-            nc.vector.tensor_tensor(reach_c[t], window(2, t, u), tr3_last[:], ALU.add)
+        def third_last(t):
+            nc.vector.tensor_tensor(third_source[t], looked_up(2, t, LAST), tr3_last[:], ALU.add)
 
-        best_of_two(u, third_last)
-        zb = tagged([P, UNIT, PACK], BF16, "zb_last", "zb%d" % (u - 1))
-        for half in (slice(0, 2), slice(2, 4)):
+        best_of_two(LAST, third_last)
+        z_bf_last = in_place_of("z_bf%d" % (LAST - 1), [P, UNIT, PACK], BF16, "z_bf_last")
+        for half in HALVES:
             for t in range(half.start, half.stop):
-                nc.vector.tensor_tensor(a[:, t, :], a[:, t, :], reach_c[t], ALU.max)
+                nc.vector.tensor_tensor(best[:, t, :], best[:, t, :], third_source[t], ALU.max)
             for t in range(half.start, half.stop):
-                nc.vector.scalar_tensor_tensor(z[:, t, :], a[:, t, :], gain[:, t : t + 1], emit_last[:, t, :], ALU.mult, ALU.add)
-        for half in (slice(0, 2), slice(2, 4)):
-            nc.vector.tensor_copy(zb[:, :, half].rearrange("p (c i) t -> p c t i", i=4), z[:, half, :].rearrange("p t (c i) -> p c t i", i=4))
-        score(zb[:].rearrange("p j t -> p (j t)"), u)
-        for q in range(4):
-            (nc.sync if q < 2 else nc.scalar).dma_start(out_2[0, 4 * q : 4 * q + 4, :].bitcast(I32), o_scales[32 * q : 32 * q + 4, :].bitcast(I32))
+                nc.vector.scalar_tensor_tensor(z_last[:, t, :], best[:, t, :], gain[:, t : t + 1], weighted_c_last[:, t, :], ALU.mult, ALU.add)
+        for half in HALVES:
+            nc.vector.tensor_copy(z_bf_last[:, :, half].rearrange("p (c i) t -> p c t i", i=4), z_last[:, half, :].rearrange("p t (c i) -> p c t i", i=4))
+        score(z_bf_last[:].rearrange("p j t -> p (j t)"), LAST)
+        for q in range(QUADRANTS):
+            queue = nc.sync if q < QUADRANTS // 2 else nc.scalar
+            queue.dma_start(out_2[0, 4 * q : 4 * q + 4, :].bitcast(I32), out_s[32 * q : 32 * q + 4, :].bitcast(I32))

from contextlib import ExitStack

import concourse.mybir as mybir
from concourse.masks import make_identity

F32 = mybir.dt.float32
BF16 = mybir.dt.bfloat16
I32 = mybir.dt.int32
U32 = mybir.dt.uint32
U16 = mybir.dt.uint16
U8 = mybir.dt.uint8
FP8X4 = mybir.dt.float8_e4m3fn_x4
ALU = mybir.AluOpType
COPY = mybir.ActivationFunctionType.Copy
RELU = mybir.ActivationFunctionType.Relu

P = 128
PACK = 4
T = 2048
S = 512
GROUP = 16
QUADRANTS = 4
UNIT = 128
UNITS = S // UNIT
LAST = UNITS - 1
TURN_BANKS = 3
PRODUCT_BANKS = 8 - TURN_BANKS
HALVES = (slice(0, 2), slice(2, 4))
OUT_SCALE = 0.0625
FLOPS = 3 * 2 * 512 * 512 * 512


def tile_picked_viterb3_none_po_kernel(tc, x_words, x_scales, w1_words, w1_scales, w2_words, w2_scales, tr1, tr2, tr3, gs, offs, two, s1, s2, s3, cand, out_0, out_1, out_2):
    nc = tc.nc

    def words_of(ap):
        return ap[0].rearrange("p n t -> p (n t)").bitcast(I32)

    def deal(dst, src):
        nc.vector.tensor_copy(dst[:].rearrange("p (t m) -> p m t", t=PACK), src[:].rearrange("p (m t) -> p m t", t=PACK))

    def places(u):
        return slice(u * UNIT, (u + 1) * UNIT)

    with ExitStack() as ctx:
        lists = ctx.enter_context(tc.tile_pool(name="lists", bufs=1))
        keep = ctx.enter_context(tc.tile_pool(name="keep", bufs=1))
        stage = ctx.enter_context(tc.tile_pool(name="stage", bufs=2))
        products = ctx.enter_context(tc.psum_pool(name="products", bufs=PRODUCT_BANKS))
        turns = ctx.enter_context(tc.psum_pool(name="turns", bufs=1))

        def new_list(name):
            return lists.tile([P, S // GROUP], U16, name=name)

        def held(shape, dtype, name):
            return keep.tile(shape, dtype, name=name, align_bytes=64)

        def in_place_of(tag, shape, dtype, name):
            return keep.tile(shape, dtype, name=name, tag=tag, align_bytes=64)

        offs_list, two_list, cand_list = new_list("offs_list"), new_list("two_list"), new_list("cand_list")
        source_lists = [new_list("s1_list"), new_list("s2_list"), new_list("s3_list")]
        x_w = held([P, T], U32, "x_w")
        x_s = held([P, T], U8, "x_s")
        w1_w, w2_w = held([P, S], U32, "w1_w"), held([P, S], U32, "w2_w")
        w1_s, w2_s = in_place_of("w1_s", [P, S], U8, "w1_s"), held([P, S], U8, "w2_s")
        tr1_all, tr2_all = held([P, S], F32, "tr1_all"), held([P, S], F32, "tr2_all")
        tr3_rows = held([P, P], F32, "tr3_rows")
        tr3_last = held([P, UNIT], F32, "tr3_last")
        gain = held([P, PACK], F32, "gain")

        def load_scales(tile, scales):
            for q in range(QUADRANTS):
                nc.sync.dma_start(tile[32 * q : 32 * q + 4, :].bitcast(I32), scales[0, 4 * q : 4 * q + 4, :].bitcast(I32))

        nc.gpsimd.memset(x_s[:].bitcast(I32), 0)
        nc.vector.memset(w1_s[:].bitcast(I32), 0)
        nc.vector.memset(w2_s[:].bitcast(I32), 0)
        nc.vector.memset(tr3_rows[:], 0.0)
        ident = held([P, P], F32, "ident")
        make_identity(nc, ident[:])

        nc.sync.dma_start(w1_w[:].bitcast(I32), words_of(w1_words))
        load_scales(x_s, x_scales)
        nc.sync.dma_start(offs_list[:], offs)
        nc.sync.dma_start(two_list[:], two)
        nc.sync.dma_start(x_w[:].bitcast(I32), words_of(x_words))
        load_scales(w1_s, w1_scales)
        nc.sync.dma_start(cand_list[:], cand)
        nc.sync.dma_start(w2_w[:].bitcast(I32), words_of(w2_words))
        nc.sync.dma_start(source_lists[0][:], s1)
        nc.sync.dma_start(tr1_all[:], tr1)
        load_scales(w2_s, w2_scales)
        nc.sync.dma_start(source_lists[1][:], s2)
        nc.sync.dma_start(tr2_all[:], tr2)
        nc.sync.dma_start(source_lists[2][:], s3)
        nc.sync.dma_start(gain[:], gs.rearrange("(p t) o -> p (t o)", t=PACK))
        nc.sync.dma_start(tr3_rows[0:LAST, :], tr3[0:1, 0 : LAST * UNIT].rearrange("o (u j) -> (o u) j", j=UNIT))
        nc.sync.dma_start(tr3_last[:], tr3[:, places(LAST)])

        offs_w = held([P, S], U32, "offs_w")
        offs_s, two_s, cand_s = held([P, S], U8, "offs_s"), held([P, S], U8, "two_s"), held([P, S], U8, "cand_s")
        w1_w_dealt = held([P, S], U32, "w1_w_dealt")
        w1_s_dealt = held([P, S], U8, "w1_s_dealt")
        cand_w_dealt = held([P, S], U32, "cand_w_dealt")
        cand_s_dealt = held([P, S], U8, "cand_s_dealt")

        deal(w1_w_dealt, w1_w)
        nc.vector.tensor_copy(offs_s[:], x_s[:].indirect(offs_list[:]))
        nc.vector.tensor_copy(two_s[:], x_s[:].indirect(two_list[:]))
        nc.vector.tensor_copy(offs_w[:], x_w[:].indirect(offs_list[:]))
        deal(w1_s_dealt, w1_s)
        two_w = in_place_of("w1_s", [P, S], U32, "two_w")
        nc.vector.tensor_copy(two_w[:], x_w[:].indirect(two_list[:]))

        y = [held([P, S], F32, "y%d" % t) for t in range(PACK)]
        for t in range(PACK):
            dealt = slice(t * P, (t + 1) * P)
            bank = products.tile([P, S], F32, name="bank")
            nc.tensor.matmul_mx(out=bank[:], lhsT=w1_w_dealt[:, dealt].bitcast(FP8X4), lhsT_scale=w1_s_dealt[:, dealt],
                                rhs=offs_w[:].bitcast(FP8X4), rhs_scale=offs_s[:], start=True, stop=True)
            nc.scalar.copy(y[t][:], bank[:])

        c_turned = {}
        for u in [LAST] + list(range(LAST)):
            bank = products.tile([P, S], F32, name="bank")
            nc.tensor.matmul_mx(out=bank[:], lhsT=two_w[:, places(u)].bitcast(FP8X4), lhsT_scale=two_s[:, places(u)],
                                rhs=w2_w[:].bitcast(FP8X4), rhs_scale=w2_s[:], start=True, stop=True)
            c_turned[u] = held([P, PACK, P], F32, "c_turned%d" % u)
            nc.scalar.copy(c_turned[u][:], bank[:].rearrange("j (p t) -> j t p", t=PACK))

        nc.vector.tensor_copy(cand_s[:], x_s[:].indirect(cand_list[:]))
        deal(cand_s_dealt, cand_s)

        bank = products.tile([P, P], F32, name="bank")
        nc.tensor.transpose(bank[:], tr3_rows[:], ident[:])
        tr3_cols = held([P, LAST], F32, "tr3_cols")
        nc.scalar.copy(tr3_cols[:], bank[:, 0:LAST])

        bank = products.tile([P, PACK, UNIT], F32, name="bank")
        weighted_c_last = held([P, PACK, UNIT], F32, "weighted_c_last")
        for t in range(PACK):
            nc.tensor.transpose(bank[:, t, :], c_turned[LAST][:, t, :], ident[:])
        for t in range(PACK):
            nc.scalar.activation(weighted_c_last[:, t, :], bank[:, t, :], COPY, scale=gain[:, t : t + 1])

        z_w = held([P, S], U32, "z_w")
        z_s = held([P, S], U8, "z_s")
        out_w = held([P, S], U32, "out_w")
        out_s = held([P, S], U8, "out_s")
        out_planes = out_0.rearrange("(p t) j -> p t j", t=PACK)
        out_words = words_of(out_1)

        def looked_up(k, t, u):
            return y[t][:].indirect(source_lists[k][:, u * UNIT // GROUP : (u + 1) * UNIT // GROUP])

        def new_room(u):
            return in_place_of("pairs%d" % max(u - 2, -1), [P, 3, PACK, UNIT], F32, "room")

        room = {0: new_room(0)}
        best_0 = held([P, PACK, UNIT], F32, "best_0")

        def best_tile(u):
            return room[u][:, 0] if u else best_0[:]

        def best_of_two(u, third):
            best, second = best_tile(u), room[u][:, 1]
            low, high = HALVES
            for t in range(PACK):
                nc.vector.tensor_tensor(best[:, t, :], looked_up(0, t, u), tr1_all[:, places(u)], ALU.add)
            for t in range(PACK - 1):
                nc.vector.tensor_tensor(second[:, t, :], looked_up(1, t, u), tr2_all[:, places(u)], ALU.add)
            nc.vector.tensor_tensor(best[:, low, :], best[:, low, :], second[:, low, :], ALU.max)
            nc.vector.tensor_tensor(second[:, PACK - 1, :], looked_up(1, PACK - 1, u), tr2_all[:, places(u)], ALU.add)
            third(0)
            nc.vector.tensor_tensor(best[:, high, :], best[:, high, :], second[:, high, :], ALU.max)
            for t in range(1, PACK):
                third(t)

        def turn_bank(number):
            return turns.tile([P, PACK, P], F32, name="turn", tag="turn%d" % (number % TURN_BANKS))

        def turn(planes, number):
            bank = turn_bank(number)
            for t in range(PACK):
                nc.tensor.transpose(bank[:, t, :], planes[:, t, :], ident[:])
            return bank

        def add_turned_back(total, term, opens, closes):
            for t in range(PACK):
                nc.tensor.matmul(total[:, t, :], term[:, t, :], ident[:], start=(opens and t == 0), stop=(closes and t == PACK - 1), is_transpose=True)

        def rounded_z(u):
            total = turn_bank(u)
            add_turned_back(total, c_turned[u], True, False)
            excess = held([P, PACK, UNIT], F32, "excess%d" % u)
            best = best_tile(u)

            def third(t):
                nc.vector.tensor_tensor(excess[:, t, :], looked_up(2, t, u), best[:, t, :], ALU.subtract)

            best_of_two(u, third)
            bank = turn(best, u - 2)
            room[u + 1] = new_room(u + 1)
            best_turned = room[u + 1][:, 2] if u else held([P, PACK, P], F32, "best_turned_0")[:]
            nc.scalar.copy(best_turned, bank[:])
            bank = turn(excess, u - 1)
            rise_turned = in_place_of("rise%d" % u, [P, PACK, P], F32, "rise_turned")
            nc.scalar.activation(rise_turned[:], bank[:], RELU, bias=tr3_cols[:, u : u + 1])
            add_turned_back(total, best_turned, False, False)
            add_turned_back(total, rise_turned, False, True)
            pairs = in_place_of("pairs%d" % u, [P, 2, UNIT, 2], BF16, "pairs")
            for e in range(2):
                for h in range(2):
                    t = 2 * h + e
                    nc.scalar.activation(pairs[:, h, :, e], total[:, t, :], COPY, scale=gain[:, t : t + 1])
            z_bf = in_place_of("z_bf%d" % u, [P, UNIT * PACK], BF16, "z_bf")
            nc.scalar.copy(z_bf[:].bitcast(F32).rearrange("p (j h) -> p j h", h=2),
                           pairs[:].rearrange("p h j e -> p (h j e)").bitcast(F32).rearrange("p (h j) -> p j h", h=2))
            return z_bf[:]

        def score(z_bf, u):
            cols = places(u)
            nc.vector.quantize_mx(out=z_w[:, cols].bitcast(FP8X4), scales=z_s[:, cols], in_=z_bf)
            bank = products.tile([P, PACK, UNIT], F32, name="bank")
            for t in range(PACK):
                dealt = slice(t * P, (t + 1) * P)
                nc.tensor.matmul_mx(out=bank[:, t, :], lhsT=cand_w_dealt[:, dealt].bitcast(FP8X4), lhsT_scale=cand_s_dealt[:, dealt],
                                    rhs=z_w[:, cols].bitcast(FP8X4), rhs_scale=z_s[:, cols], start=True, stop=True)
            out_bf = held([P, UNIT, PACK], BF16, "out_bf%d" % u)
            nc.scalar.activation(out_bf[:], bank[:].rearrange("p t j -> p j t"), COPY, scale=OUT_SCALE)
            out_f32 = stage.tile([P, PACK, UNIT], F32, name="out_f32")
            pieces = ((nc.sync, HALVES[0]), (nc.scalar, HALVES[1])) if u == LAST else ((nc.sync, slice(0, PACK)),)
            for queue, planes in pieces:
                nc.scalar.activation(out_f32[:, planes, :], bank[:, planes, :], COPY, scale=OUT_SCALE)
                queue.dma_start(out_planes[:, planes, cols], out_f32[:, planes, :])
            nc.vector.quantize_mx(out=out_w[:, cols].bitcast(FP8X4), scales=out_s[:, cols], in_=out_bf[:].rearrange("p j t -> p (j t)"))
            nc.sync.dma_start(out_words[:, cols], out_w[:, cols].bitcast(I32))

        z_bf_0 = rounded_z(0)
        cand_w = in_place_of("rise0", [P, S], U32, "cand_w")
        nc.vector.tensor_copy(cand_w[:], x_w[:].indirect(cand_list[:]))
        deal(cand_w_dealt, cand_w)
        score(z_bf_0, 0)
        for u in range(1, LAST):
            score(rounded_z(u), u)

        best = best_tile(LAST)
        z_last = held([P, PACK, UNIT], F32, "z_last")
        late = in_place_of("pairs%d" % (LAST - 1), [P, 2, UNIT], F32, "late")
        third_source = [room[LAST][:, 1, 0, :], room[LAST][:, 1, 1, :], late[:, 0, :], late[:, 1, :]]

        def third_last(t):
            nc.vector.tensor_tensor(third_source[t], looked_up(2, t, LAST), tr3_last[:], ALU.add)

        best_of_two(LAST, third_last)
        z_bf_last = in_place_of("z_bf%d" % (LAST - 1), [P, UNIT, PACK], BF16, "z_bf_last")
        for half in HALVES:
            for t in range(half.start, half.stop):
                nc.vector.tensor_tensor(best[:, t, :], best[:, t, :], third_source[t], ALU.max)
            for t in range(half.start, half.stop):
                nc.vector.scalar_tensor_tensor(z_last[:, t, :], best[:, t, :], gain[:, t : t + 1], weighted_c_last[:, t, :], ALU.mult, ALU.add)
        for half in HALVES:
            nc.vector.tensor_copy(z_bf_last[:, :, half].rearrange("p (c i) t -> p c t i", i=4), z_last[:, half, :].rearrange("p t (c i) -> p c t i", i=4))
        score(z_bf_last[:].rearrange("p j t -> p (j t)"), LAST)
        for q in range(QUADRANTS):
            queue = nc.sync if q < QUADRANTS // 2 else nc.scalar
            queue.dma_start(out_2[0, 4 * q : 4 * q + 4, :].bitcast(I32), out_s[32 * q : 32 * q + 4, :].bitcast(I32))
